import numpy as np
import ml_dtypes


def mxq(x, axis, fmt="e4m3"):
    dtype, down = {"e4m3": (ml_dtypes.float8_e4m3fn, 7), "e5m2": (ml_dtypes.float8_e5m2, 14)}[fmt]
    v = np.moveaxis(np.asarray(x, np.float32).astype(ml_dtypes.bfloat16).astype(np.float64), axis, -1)
    blocks = v.reshape(v.shape[:-1] + (-1, 32))
    amax = np.abs(blocks).max(-1, keepdims=True)
    byte = np.maximum(np.where(amax > 0, np.frexp(amax)[1] - 1 + 127, 0) - down, 1)
    scale = np.exp2(byte - 127.0)
    codes = (blocks / scale).astype(np.float32).astype(dtype).astype(np.float64)
    return np.moveaxis((codes * scale).reshape(v.shape), -1, axis)


WIDE = False


def mx_kscale(k):
    if not WIDE:
        return np.ones(k)
    levels = np.array([10, -10, 5, -5, 0])
    if k % 512:
        return np.exp2(np.random.permutation(np.resize(levels, k // 32))).repeat(32)
    a = np.empty((k // 512, 16))
    for p in range(k // 512):
        a[p, :8] = np.random.permutation(np.resize(levels, 8))
        for g in range(8):
            far = levels[np.abs(levels - a[p, g]) >= 10]
            a[p, g + 8] = far[np.random.randint(len(far))]
    return np.exp2(a.ravel()).repeat(32)


def f64(x):
    return np.asarray(x).astype(np.float64)


def striped(idx):
    return np.tile(idx.reshape(-1, 16).T, (8, 1)).astype(np.uint16)


def unstriped(offs):
    return offs[:16].T.reshape(-1).astype(np.int64)


def striped8(idx):
    return np.concatenate([x.reshape(-1, 16).T for x in idx]).astype(np.uint16)


def runs(offs, k):
    lists = np.stack([offs[16 * r : 16 * r + 16].T.reshape(-1) for r in range(8)]).astype(np.int64)
    return lists[np.arange(k) % 512 // 64]


def pack_weight(w):
    k, n = w.shape
    w = f64(np.asarray(w, np.float32).astype(ml_dtypes.bfloat16)).reshape(k // 32, 32, n)
    amax = np.abs(w).max(1)
    byte = np.clip(np.where(amax > 0, np.frexp(amax)[1] - 1 + 127 - 7, 1), 1, 254)
    scaled = (w * np.exp2(127.0 - byte)[:, None, :]).reshape(k, n).astype(np.float32)
    words = np.ascontiguousarray(scaled.reshape(k // 512, 128, 4, n).transpose(0, 1, 3, 2)).astype(ml_dtypes.float8_e4m3fn).view(np.uint8)
    return words, np.ascontiguousarray(byte.astype(np.uint8).reshape(k // 512, 16, n))


def unpack_weight(words, scales):
    g, p, n, _ = words.shape
    vals = np.ascontiguousarray(words).view(ml_dtypes.float8_e4m3fn).astype(np.float64) * np.repeat(np.exp2(scales.astype(np.float64) - 127.0), 8, axis=1)[..., None]
    return vals.transpose(0, 1, 3, 2).reshape(g * 512, n)

def planes(y):
    n, m = y.shape
    v = y.astype(np.float32).astype(ml_dtypes.bfloat16).astype(np.float64).reshape(n // 32, 32, m)
    top = np.abs(v).max(1)
    byte = np.clip(np.where(top > 0, np.frexp(top)[1] - 1 + 127 - 7, 1), 1, 254)
    codes = (v * np.exp2(127.0 - byte)[:, None, :]).reshape(n, m).astype(np.float32).astype(ml_dtypes.float8_e4m3fn).view(np.uint8)
    words = codes.reshape(n // 512, 128, 4, m).transpose(0, 1, 3, 2)
    return np.ascontiguousarray(words), np.ascontiguousarray(byte.astype(np.uint8).reshape(n // 512, 16, m))


K, T, S, N, H, G = 512, 2048, 512, 512, 512, 2048


def setup_inputs():
    n = np.random.standard_normal
    s = mx_kscale(K)[:, None]
    u = mx_kscale(S)
    packed_xT = pack_weight(n((K, T)) * s)
    packed_w1 = pack_weight(n((K, H)) / np.sqrt(K) / s)
    packed_dT = pack_weight(n((K, G)) / s)
    packed_w2 = pack_weight(n((H, N)) / np.sqrt(H) / u[:, None])
    return {
        "x_words": packed_xT[0],
        "x_scales": packed_xT[1],
        "w1_words": packed_w1[0],
        "w1_scales": packed_w1[1],
        "d_words": packed_dT[0],
        "d_scales": packed_dT[1],
        "gn": (np.random.uniform(0.5, 1.5, (H, 1)) * u[:, None]).astype(np.float32),
        "w2_words": packed_w2[0],
        "w2_scales": packed_w2[1],
        "tau": np.random.uniform(0.3, 0.9, (N, 1)).astype(np.float32),
        "offs": striped(np.random.permutation(T)[:S]),
        "k1": striped8(np.random.randint(0, G, (8, H))),
        "two": striped(np.random.permutation(T)[:S]),
        "n1": striped(np.random.permutation(S)),
        "n2": striped(np.random.permutation(S)),
        "n3": striped(np.random.permutation(S)),
        "n4": striped(np.random.permutation(S)),
    }


def reference(x_words, x_scales, w1_words, w1_scales, d_words, d_scales, gn, w2_words, w2_scales, tau, offs, k1, two, n1, n2, n3, n4):
    xq = unpack_weight(x_words, x_scales)[:, unstriped(offs)]
    y = unpack_weight(w1_words, w1_scales).T @ xq
    d_k1 = unpack_weight(d_words, d_scales)[np.arange(K)[:, None], runs(k1, K)]
    x_two = unpack_weight(x_words, x_scales)[:, unstriped(two)]
    d = 0.0625 * (d_k1.T @ x_two)
    z = f64(gn) * (0.75 * (y * d[:, unstriped(n2)] - (y[:, unstriped(n1)] * d)))
    h = unpack_weight(w2_words, w2_scales).T @ mxq(z, 0, "e4m3")
    top = h.max(axis=1, keepdims=True)
    ea = np.exp(f64(tau) * (h[:, unstriped(n3)] - top))
    out_0 = np.maximum(h, 2.0 * ea) - (0.5 * h[:, unstriped(n4)])
    return (out_0,) + planes(out_0)

@@ -1,0 +1,216 @@
+from contextlib import ExitStack
+
+import concourse.mybir as mybir
+
+F32 = mybir.dt.float32
+BF16 = mybir.dt.bfloat16
+I32 = mybir.dt.int32
+U32 = mybir.dt.uint32
+U16 = mybir.dt.uint16
+U8 = mybir.dt.uint8
+FP8X4 = mybir.dt.float8_e4m3fn_x4
+ALU = mybir.AluOpType
+ACT = mybir.ActivationFunctionType
+
+P = 128
+PACK = 4
+S = 512
+T = 2048
+HALF = S // 2
+LIST_COLS = S // 16
+FLOPS = 3 * 2 * 512 * 512 * 512
+
+
+def tile_picked_twkeycrossbecl_none_po_kernel(
+    tc, x_words, x_scales, w1_words, w1_scales, d_words, d_scales, gn, w2_words, w2_scales, tau,
+    offs, k1, two, n1, n2, n3, n4, out_0, out_1, out_2,
+):
+    nc = tc.nc
+    halves = [slice(c * HALF, (c + 1) * HALF) for c in range(2)]
+    list_halves = [slice(c * LIST_COLS // 2, (c + 1) * LIST_COLS // 2) for c in range(2)]
+
+    with ExitStack() as ctx:
+        keep = ctx.enter_context(tc.tile_pool(name="keep", bufs=1))
+        psum = ctx.enter_context(tc.psum_pool(name="psum", bufs=1))
+
+        def tile(shape, dtype, name):
+            return keep.tile(shape, dtype, name=name, align_bytes=64)
+
+        def load_list(src, name):
+            dst = keep.tile([P, LIST_COLS], U16, name=name)
+            nc.sync.dma_start(dst[:], src)
+            return dst
+
+        def load_words(src, width, name):
+            dst = tile([P, width], U32, name)
+            nc.sync.dma_start(dst[:].bitcast(I32), src[0].rearrange("p n t -> p (n t)").bitcast(I32))
+            return dst
+
+        def zeroed_plane(width, name, engine):
+            dst = tile([P, width], U8, name)
+            engine.memset(dst[:].bitcast(I32), 0)
+            return dst
+
+        def load_scale_rows(queue, dst, src):
+            for q in range(4):
+                queue.dma_start(dst[32 * q : 32 * q + 4, :].bitcast(I32), src[0, 4 * q : 4 * q + 4, :].bitcast(I32))
+
+        def dealt(ap):
+            return ap.rearrange("p (m t) -> p t m", t=PACK)
+
+        def as_dealt(ap):
+            return ap.rearrange("p (t m) -> p t m", t=PACK)
+
+        def mm(out, lw, ls, t, rw, rs):
+            cols = slice(t * P, (t + 1) * P)
+            nc.tensor.matmul_mx(out=out, lhsT=lw[:, cols].bitcast(FP8X4), lhsT_scale=ls[:, cols],
+                                rhs=rw.bitcast(FP8X4), rhs_scale=rs, start=True, stop=True)
+
+        xs_table = zeroed_plane(T, "xs_table", nc.gpsimd)
+        ds_table = zeroed_plane(T, "ds_table", nc.vector)
+        w1s_raw = zeroed_plane(S, "w1s_raw", nc.vector)
+        ds_placed = zeroed_plane(S, "ds_placed", nc.vector)
+        w2s_raw = zeroed_plane(S, "w2s_raw", nc.vector)
+
+        gn_sb = tile([P, PACK], F32, "gn_sb")
+        nc.gpsimd.dma_start(gn_sb[:], gn.rearrange("(p t) o -> p (t o)", t=PACK))
+        tau_sb = tile([P, PACK], F32, "tau_sb")
+        nc.gpsimd.dma_start(tau_sb[:], tau.rearrange("(p t) o -> p (t o)", t=PACK))
+
+        offs_sb = load_list(offs, "offs_sb")
+        k1_sb = load_list(k1, "k1_sb")
+        load_scale_rows(nc.sync, xs_table, x_scales)
+        nc.sync.dma_start(ds_table[0:P:8, :].bitcast(I32), d_scales[0].bitcast(I32))
+        xw_table = load_words(x_words, T, "xw_table")
+        w1w_raw = load_words(w1_words, S, "w1w_raw")
+        load_scale_rows(nc.sync, w1s_raw, w1_scales)
+        two_sb = load_list(two, "two_sb")
+        dw_table = load_words(d_words, T, "dw_table")
+        n1_sb = load_list(n1, "n1_sb")
+        n2_sb = load_list(n2, "n2_sb")
+        w2w_raw = load_words(w2_words, S, "w2w_raw")
+        load_scale_rows(nc.gpsimd, w2s_raw, w2_scales)
+        n4_sb = load_list(n4, "n4_sb")
+        n3_sb = load_list(n3, "n3_sb")
+
+        gain = tile([P, PACK], F32, "gain")
+        nc.scalar.activation(gain[:], gn_sb[:], ACT.Copy, scale=0.75 * 0.0625)
+
+        xs_idx = tile([P, S], U8, "xs_idx")
+        nc.vector.tensor_copy(xs_idx[:], xs_table[:].indirect(offs_sb[:]))
+        ds_k1 = tile([P, S], U8, "ds_k1")
+        nc.vector.tensor_copy(ds_k1[:], ds_table[:].indirect(k1_sb[:]))
+        w1w = tile([P, S], U32, "w1w")
+        nc.scalar.copy(as_dealt(w1w[:]), dealt(w1w_raw[:]))
+        xw_idx = tile([P, S], U32, "xw_idx")
+        nc.vector.tensor_copy(xw_idx[:], xw_table[:].indirect(offs_sb[:]))
+        w1s = tile([P, S], U8, "w1s")
+        nc.vector.tensor_copy(as_dealt(w1s[:]), dealt(w1s_raw[:]))
+
+        y_ps = [psum.tile([P, S], F32, name="y_ps%d" % t, tag="bank%d" % t) for t in range(PACK)]
+        y = [tile([P, S], F32, "y%d" % t) for t in range(PACK)]
+        for t in range(PACK):
+            mm(y_ps[t][:], w1w, w1s, t, xw_idx[:], xs_idx[:])
+        for t in range(PACK):
+            nc.scalar.copy(y[t][:], y_ps[t][:])
+
+        ds_dealt = tile([P, S], U8, "ds_dealt")
+        nc.vector.tensor_copy(as_dealt(ds_dealt[:]), dealt(ds_k1[:]))
+        for r in range(4):
+            nc.sync.dma_start(ds_placed[r:P:32, :].bitcast(I32), ds_dealt[8 * r : P : 32, :].bitcast(I32))
+        xs_two = tile([P, S], U8, "xs_two")
+        nc.vector.tensor_copy(xs_two[:], xs_table[:].indirect(two_sb[:]))
+        xw_two = tile([P, S], U32, "xw_two")
+        nc.vector.tensor_copy(xw_two[:], xw_table[:].indirect(two_sb[:]))
+        dw_k1 = tile([P, S], U32, "dw_k1")
+        nc.vector.tensor_copy(dw_k1[:], dw_table[:].indirect(k1_sb[:]))
+        dw = tile([P, S], U32, "dw")
+        nc.vector.tensor_copy(as_dealt(dw[:]), dealt(dw_k1[:]))
+        w2w = tile([P, S], U32, "w2w")
+        nc.vector.tensor_copy(as_dealt(w2w[:]), dealt(w2w_raw[:]))
+        w2s = tile([P, S], U8, "w2s")
+        nc.vector.tensor_copy(as_dealt(w2s[:]), dealt(w2s_raw[:]))
+
+        d_ps = [psum.tile([P, S], F32, name="d_ps%d" % t, tag="bank%d" % (PACK + t)) for t in range(PACK)]
+        for t in range(PACK):
+            mm(d_ps[t][:], dw, ds_placed, t, xw_two[:], xs_two[:])
+
+        y_n1 = [tile([P, S], F32, "y_n1_%d" % t) for t in range(PACK)]
+        d = [tile([P, S], F32, "d%d" % t) for t in range(PACK)]
+        d_n2 = [[tile([P, HALF], F32, "d_n2_%d_%d" % (t, c)) for c in range(2)] for t in range(1, PACK)]
+        left = [tile([P, PACK, HALF], F32, "left%d" % c) for c in range(2)]
+        right = [tile([P, PACK, HALF], F32, "right%d" % c) for c in range(2)]
+
+        def fetch_y(t):
+            for c in range(2):
+                nc.scalar.activation(y_n1[t][:, halves[c]], y[t][:].indirect(n1_sb[:, list_halves[c]]), ACT.Copy)
+
+        def make_right(t):
+            for c in range(2):
+                nc.vector.tensor_tensor(right[c][:, t, :], y_n1[t][:, halves[c]], d[t][:, halves[c]], ALU.mult)
+
+        for t in range(PACK - 1):
+            fetch_y(t)
+        nc.vector.tensor_scalar(d[0][:], d_ps[0][:], gain[:, 0:1], None, ALU.mult)
+        nc.scalar.activation(d[1][:], d_ps[1][:], ACT.Copy, scale=gain[:, 1:2])
+        for c in range(2):
+            nc.vector.tensor_tensor(left[c][:, 0, :], d[0][:].indirect(n2_sb[:, list_halves[c]]), y[0][:, halves[c]], ALU.mult)
+        make_right(0)
+        for t in range(2, PACK):
+            nc.scalar.activation(d[t][:], d_ps[t][:], ACT.Copy, scale=gain[:, t : t + 1])
+        fetch_y(PACK - 1)
+        for t in range(1, PACK):
+            make_right(t)
+
+        h_ps = [[psum.tile([P, S], F32, name="h_ps%d_%d" % (c, t), tag="bank%d" % (PACK * c + t)) for t in range(PACK)] for c in range(2)]
+        for c in range(2):
+            for t in range(1, PACK):
+                nc.scalar.activation(d_n2[t - 1][c][:], d[t][:].indirect(n2_sb[:, list_halves[c]]), ACT.Copy)
+                nc.vector.tensor_tensor(left[c][:, t, :], d_n2[t - 1][c][:], y[t][:, halves[c]], ALU.mult)
+            z = tile([P, HALF, PACK], BF16, "z%d" % c)
+            nc.vector.tensor_tensor(
+                z[:].rearrange("p (g i) t -> p g t i", i=4),
+                left[c][:].rearrange("p t (g i) -> p g t i", i=4),
+                right[c][:].rearrange("p t (g i) -> p g t i", i=4),
+                ALU.subtract,
+            )
+            zw = tile([P, HALF], U32, "zw%d" % c)
+            zs = tile([P, HALF], U8, "zs%d" % c)
+            nc.vector.quantize_mx(out=zw[:].bitcast(FP8X4), scales=zs[:], in_=z[:].rearrange("p j t -> p (j t)"))
+            for t in range(PACK):
+                mm(h_ps[c][t][:, halves[0]], w2w, w2s, t, zw[:], zs[:])
+
+        h = [tile([P, S], F32, "h%d" % t) for t in range(PACK)]
+        top0 = [tile([P, 1], F32, "top0_%d" % t) for t in range(PACK)]
+        top = [tile([P, 1], F32, "top_%d" % t) for t in range(PACK)]
+        shift = [tile([P, 1], F32, "shift_%d" % t) for t in range(PACK)]
+        for t in range(PACK):
+            nc.vector.tensor_scalar(h[t][:, halves[0]], h_ps[0][t][:, halves[0]], 1.0, None, ALU.mult, ALU.max, accum_out=top0[t][:])
+        for t in range(PACK):
+            nc.vector.tensor_scalar(h[t][:, halves[1]], h_ps[1][t][:, halves[0]], 1.0, top0[t][:], ALU.mult, ALU.max, accum_out=top[t][:])
+            nc.gpsimd.tensor_scalar(shift[t][:], top[t][:], tau_sb[:, t : t + 1], -1.0, ALU.mult, ALU.mult)
+
+        out_rows = out_0.rearrange("(p t) j -> p t j", t=PACK)
+        out_words = out_1[0].rearrange("p n t -> p (n t)").bitcast(I32)
+        ow = tile([P, S], U32, "ow")
+        osc = tile([P, S], U8, "osc")
+        for c in range(2):
+            res = tile([P, PACK, HALF], F32, "res%d" % c)
+            for t in range(PACK):
+                h_n4 = tile([P, HALF], F32, "h_n4_%d_%d" % (t, c))
+                ea = tile([P, HALF], F32, "ea_%d_%d" % (t, c))
+                big = tile([P, HALF], F32, "big_%d_%d" % (t, c))
+                nc.scalar.activation(h_n4[:], h[t][:].indirect(n4_sb[:, list_halves[c]]), ACT.Copy)
+                nc.scalar.activation(ea[:], h[t][:].indirect(n3_sb[:, list_halves[c]]), ACT.Exp,
+                                     bias=shift[t][:], scale=tau_sb[:, t : t + 1])
+                nc.vector.scalar_tensor_tensor(big[:], ea[:], 2.0, h_ps[c][t][:, halves[0]], ALU.mult, ALU.max)
+                nc.vector.scalar_tensor_tensor(res[:, t, :], h_n4[:], -0.5, big[:], ALU.mult, ALU.add)
+            nc.sync.dma_start(out_rows[:, :, halves[c]], res[:])
+            res_bf = tile([P, HALF, PACK], BF16, "res_bf%d" % c)
+            nc.vector.tensor_copy(res_bf[:].rearrange("p (g i) t -> p g t i", i=4), res[:].rearrange("p t (g i) -> p g t i", i=4))
+            nc.vector.quantize_mx(out=ow[:, halves[c]].bitcast(FP8X4), scales=osc[:, halves[c]],
+                                  in_=res_bf[:].rearrange("p j t -> p (j t)"))
+            nc.sync.dma_start(out_words[:, halves[c]], ow[:, halves[c]].bitcast(I32))
+        for q in range(4):
+            queue = nc.scalar if q % 2 else nc.sync
+            queue.dma_start(out_2[0, 4 * q : 4 * q + 4, :].bitcast(I32), osc[32 * q : 32 * q + 4, :].bitcast(I32))

@@ -33,8 +33,8 @@ def tile_picked_twkeycrossbecl_none_po_kernel(
         keep = ctx.enter_context(tc.tile_pool(name="keep", bufs=1))
         psum = ctx.enter_context(tc.psum_pool(name="psum", bufs=1))
 
-        def tile(shape, dtype, name):
-            return keep.tile(shape, dtype, name=name, align_bytes=64)
+        def tile(shape, dtype, name, tag=None):
+            return keep.tile(shape, dtype, name=name, tag=tag or name, align_bytes=64)
 
         def load_list(src, name):
             dst = keep.tile([P, LIST_COLS], U16, name=name)
@@ -46,8 +46,8 @@ def tile_picked_twkeycrossbecl_none_po_kernel(
             nc.sync.dma_start(dst[:].bitcast(I32), src[0].rearrange("p n t -> p (n t)").bitcast(I32))
             return dst
 
-        def zeroed_plane(width, name, engine):
-            dst = tile([P, width], U8, name)
+        def zeroed_plane(width, name, engine, tag=None):
+            dst = tile([P, width], U8, name, tag)
             engine.memset(dst[:].bitcast(I32), 0)
             return dst
 
@@ -66,9 +66,8 @@ def tile_picked_twkeycrossbecl_none_po_kernel(
             nc.tensor.matmul_mx(out=out, lhsT=lw[:, cols].bitcast(FP8X4), lhsT_scale=ls[:, cols],
                                 rhs=rw.bitcast(FP8X4), rhs_scale=rs, start=True, stop=True)
 
-        xs_table = zeroed_plane(T, "xs_table", nc.gpsimd)
-        ds_table = zeroed_plane(T, "ds_table", nc.vector)
-        w1s_raw = zeroed_plane(S, "w1s_raw", nc.vector)
+        ds_table = zeroed_plane(T, "ds_table", nc.gpsimd)
+        w1s_raw = zeroed_plane(S, "w1s_raw", nc.vector, "relay")
         ds_placed = zeroed_plane(S, "ds_placed", nc.vector)
         w2s_raw = zeroed_plane(S, "w2s_raw", nc.vector)
 
@@ -78,8 +77,11 @@ def tile_picked_twkeycrossbecl_none_po_kernel(
         nc.gpsimd.dma_start(tau_sb[:], tau.rearrange("(p t) o -> p (t o)", t=PACK))
 
         offs_sb = load_list(offs, "offs_sb")
+        xs_table = tile([P, T], U8, "xs_table")
+        for q in range(4):
+            nc.sync.dma_start(xs_table[32 * q : 32 * q + 32, :].bitcast(I32),
+                              x_scales[0, 4 * q : 4 * q + 4, :].bitcast(I32).partition_broadcast(8))
         k1_sb = load_list(k1, "k1_sb")
-        load_scale_rows(nc.sync, xs_table, x_scales)
         nc.sync.dma_start(ds_table[0:P:8, :].bitcast(I32), d_scales[0].bitcast(I32))
         xw_table = load_words(x_words, T, "xw_table")
         w1w_raw = load_words(w1_words, S, "w1w_raw")
@@ -89,9 +91,9 @@ def tile_picked_twkeycrossbecl_none_po_kernel(
         n1_sb = load_list(n1, "n1_sb")
         n2_sb = load_list(n2, "n2_sb")
         w2w_raw = load_words(w2_words, S, "w2w_raw")
-        load_scale_rows(nc.gpsimd, w2s_raw, w2_scales)
-        n4_sb = load_list(n4, "n4_sb")
         n3_sb = load_list(n3, "n3_sb")
+        n4_sb = load_list(n4, "n4_sb")
+        load_scale_rows(nc.sync, w2s_raw, w2_scales)
 
         gain = tile([P, PACK], F32, "gain")
         nc.scalar.activation(gain[:], gn_sb[:], ACT.Copy, scale=0.75 * 0.0625)
@@ -105,16 +107,18 @@ def tile_picked_twkeycrossbecl_none_po_kernel(
         xw_idx = tile([P, S], U32, "xw_idx")
         nc.vector.tensor_copy(xw_idx[:], xw_table[:].indirect(offs_sb[:]))
         w1s = tile([P, S], U8, "w1s")
-        nc.vector.tensor_copy(as_dealt(w1s[:]), dealt(w1s_raw[:]))
+        nc.gpsimd.tensor_copy(as_dealt(w1s[:]), dealt(w1s_raw[:]))
 
         y_ps = [psum.tile([P, S], F32, name="y_ps%d" % t, tag="bank%d" % t) for t in range(PACK)]
-        y = [tile([P, S], F32, "y%d" % t) for t in range(PACK)]
+        y = [tile([P, S + 16], F32, "y%d" % t) for t in range(PACK)]
+        for t in range(PACK):
+            nc.vector.memset(y[t][:, S:], 0.0)
         for t in range(PACK):
             mm(y_ps[t][:], w1w, w1s, t, xw_idx[:], xs_idx[:])
         for t in range(PACK):
-            nc.scalar.copy(y[t][:], y_ps[t][:])
+            nc.scalar.copy(y[t][:, :S], y_ps[t][:])
 
-        ds_dealt = tile([P, S], U8, "ds_dealt")
+        ds_dealt = tile([P, S], U8, "ds_dealt", "relay")
         nc.vector.tensor_copy(as_dealt(ds_dealt[:]), dealt(ds_k1[:]))
         for r in range(4):
             nc.sync.dma_start(ds_placed[r:P:32, :].bitcast(I32), ds_dealt[8 * r : P : 32, :].bitcast(I32))
@@ -127,9 +131,10 @@ def tile_picked_twkeycrossbecl_none_po_kernel(
         dw = tile([P, S], U32, "dw")
         nc.vector.tensor_copy(as_dealt(dw[:]), dealt(dw_k1[:]))
         w2w = tile([P, S], U32, "w2w")
-        nc.vector.tensor_copy(as_dealt(w2w[:]), dealt(w2w_raw[:]))
+        nc.gpsimd.tensor_copy(as_dealt(w2w[:]), dealt(w2w_raw[:]))
+
         w2s = tile([P, S], U8, "w2s")
-        nc.vector.tensor_copy(as_dealt(w2s[:]), dealt(w2s_raw[:]))
+        nc.gpsimd.tensor_copy(as_dealt(w2s[:]), dealt(w2s_raw[:]))
 
         d_ps = [psum.tile([P, S], F32, name="d_ps%d" % t, tag="bank%d" % (PACK + t)) for t in range(PACK)]
         for t in range(PACK):
@@ -137,79 +142,129 @@ def tile_picked_twkeycrossbecl_none_po_kernel(
 
         y_n1 = [tile([P, S], F32, "y_n1_%d" % t) for t in range(PACK)]
         d = [tile([P, S], F32, "d%d" % t) for t in range(PACK)]
-        d_n2 = [[tile([P, HALF], F32, "d_n2_%d_%d" % (t, c)) for c in range(2)] for t in range(1, PACK)]
-        left = [tile([P, PACK, HALF], F32, "left%d" % c) for c in range(2)]
+        d_n2 = {(t, c): tile([P, HALF], F32, "d_n2_%d_%d" % (t, c), "d_n2_%d" % (t + c)) for c in range(2) for t in range(1 - c, PACK)}
+        left = [tile([P, PACK, HALF], F32, "left%d" % c, "left") for c in range(2)]
         right = [tile([P, PACK, HALF], F32, "right%d" % c) for c in range(2)]
 
         def fetch_y(t):
-            for c in range(2):
-                nc.scalar.activation(y_n1[t][:, halves[c]], y[t][:].indirect(n1_sb[:, list_halves[c]]), ACT.Copy)
+            nc.scalar.activation(y_n1[t][:], y[t][:].indirect(n1_sb[:]), ACT.Copy)
 
-        def make_right(t):
-            for c in range(2):
-                nc.vector.tensor_tensor(right[c][:, t, :], y_n1[t][:, halves[c]], d[t][:, halves[c]], ALU.mult)
-
-        for t in range(PACK - 1):
+        for t in range(PACK):
             fetch_y(t)
-        nc.vector.tensor_scalar(d[0][:], d_ps[0][:], gain[:, 0:1], None, ALU.mult)
-        nc.scalar.activation(d[1][:], d_ps[1][:], ACT.Copy, scale=gain[:, 1:2])
-        for c in range(2):
-            nc.vector.tensor_tensor(left[c][:, 0, :], d[0][:].indirect(n2_sb[:, list_halves[c]]), y[0][:, halves[c]], ALU.mult)
-        make_right(0)
-        for t in range(2, PACK):
-            nc.scalar.activation(d[t][:], d_ps[t][:], ACT.Copy, scale=gain[:, t : t + 1])
-        fetch_y(PACK - 1)
-        for t in range(1, PACK):
-            make_right(t)
+        for t in range(PACK):
+            nc.vector.tensor_scalar(d[t][:], d_ps[t][:], gain[:, t : t + 1], None, ALU.mult)
+            nc.gpsimd.tensor_tensor(right[1][:, t, :], y_n1[t][:, halves[1]], d[t][:, halves[1]], ALU.mult)
+        for t in range(PACK):
+            nc.vector.scalar_tensor_tensor(right[0][:, t, :], d_ps[t][:, halves[0]], gain[:, t : t + 1],
+                                           y_n1[t][:, halves[0]], ALU.mult, ALU.mult)
 
-        h_ps = [[psum.tile([P, S], F32, name="h_ps%d_%d" % (c, t), tag="bank%d" % (PACK * c + t)) for t in range(PACK)] for c in range(2)]
-        for c in range(2):
-            for t in range(1, PACK):
-                nc.scalar.activation(d_n2[t - 1][c][:], d[t][:].indirect(n2_sb[:, list_halves[c]]), ACT.Copy)
-                nc.vector.tensor_tensor(left[c][:, t, :], d_n2[t - 1][c][:], y[t][:, halves[c]], ALU.mult)
-            z = tile([P, HALF, PACK], BF16, "z%d" % c)
+        h_ps = [psum.tile([P, S], F32, name="h_ps%d" % t, tag="bank%d" % (PACK + t)) for t in range(PACK)]
+        z = [tile([P, HALF, PACK], BF16, "z%d" % c) for c in range(2)]
+        zw = [tile([P, HALF], U32, "zw%d" % c) for c in range(2)]
+        zs = [tile([P, HALF], U8, "zs%d" % c) for c in range(2)]
+
+        def make_left(t, c):
+            nc.scalar.activation(d_n2[t, c][:], d[t][:].indirect(n2_sb[:, list_halves[c]]), ACT.Copy)
+            nc.vector.tensor_tensor(left[c][:, t, :], d_n2[t, c][:], y_ps[t][:, halves[c]], ALU.mult)
+
+        def make_z(c):
             nc.vector.tensor_tensor(
-                z[:].rearrange("p (g i) t -> p g t i", i=4),
+                z[c][:].rearrange("p (g i) t -> p g t i", i=4),
                 left[c][:].rearrange("p t (g i) -> p g t i", i=4),
                 right[c][:].rearrange("p t (g i) -> p g t i", i=4),
                 ALU.subtract,
             )
-            zw = tile([P, HALF], U32, "zw%d" % c)
-            zs = tile([P, HALF], U8, "zs%d" % c)
-            nc.vector.quantize_mx(out=zw[:].bitcast(FP8X4), scales=zs[:], in_=z[:].rearrange("p j t -> p (j t)"))
+
+        def second_product(c):
+            nc.vector.quantize_mx(out=zw[c][:].bitcast(FP8X4), scales=zs[c][:], in_=z[c][:].rearrange("p j t -> p (j t)"))
             for t in range(PACK):
-                mm(h_ps[c][t][:, halves[0]], w2w, w2s, t, zw[:], zs[:])
+                mm(h_ps[t][:, halves[c]], w2w, w2s, t, zw[c][:], zs[c][:])
 
         h = [tile([P, S], F32, "h%d" % t) for t in range(PACK)]
-        top0 = [tile([P, 1], F32, "top0_%d" % t) for t in range(PACK)]
+        top_half = [tile([P, 1], F32, "top_half_%d" % t) for t in range(2)]
         top = [tile([P, 1], F32, "top_%d" % t) for t in range(PACK)]
         shift = [tile([P, 1], F32, "shift_%d" % t) for t in range(PACK)]
-        for t in range(PACK):
-            nc.vector.tensor_scalar(h[t][:, halves[0]], h_ps[0][t][:, halves[0]], 1.0, None, ALU.mult, ALU.max, accum_out=top0[t][:])
-        for t in range(PACK):
-            nc.vector.tensor_scalar(h[t][:, halves[1]], h_ps[1][t][:, halves[0]], 1.0, top0[t][:], ALU.mult, ALU.max, accum_out=top[t][:])
-            nc.gpsimd.tensor_scalar(shift[t][:], top[t][:], tau_sb[:, t : t + 1], -1.0, ALU.mult, ALU.mult)
+
+        def take_h(t, cols, so_far, largest):
+            nc.vector.tensor_scalar(h[t][:, cols], h_ps[t][:, cols], 1.0, so_far, ALU.mult, ALU.max, accum_out=largest)
+
+        def make_shift(t):
+            nc.vector.tensor_scalar(shift[t][:], top[t][:], tau_sb[:, t : t + 1], -1.0, ALU.mult, ALU.mult)
+
+        nc.vector.tensor_tensor(left[0][:, 0, :], d[0][:].indirect(n2_sb[:, list_halves[0]]), y[0][:, halves[0]], ALU.mult)
+        for t in range(1, PACK):
+            make_left(t, 0)
+        make_z(0)
+        make_left(0, 1)
+        second_product(0)
+        for t in range(1, PACK):
+            make_left(t, 1)
+        take_h(0, halves[0], None, top_half[0][:])
+        make_z(1)
+        take_h(1, halves[0], None, top_half[1][:])
+        second_product(1)
+        take_h(0, halves[1], top_half[0][:], top[0][:])
+        take_h(1, halves[1], top_half[1][:], top[1][:])
+        make_shift(0)
+        take_h(2, slice(0, S), None, top[2][:])
+        make_shift(1)
+        take_h(3, slice(0, S), None, top[3][:])
+        make_shift(2)
+        make_shift(3)
 
         out_rows = out_0.rearrange("(p t) j -> p t j", t=PACK)
         out_words = out_1[0].rearrange("p n t -> p (n t)").bitcast(I32)
         ow = tile([P, S], U32, "ow")
         osc = tile([P, S], U8, "osc")
+        res = [tile([P, PACK, HALF], F32, "res%d" % c) for c in range(2)]
+
+        def fetch_h(t, c, lo, hi, engine):
+            h_n4 = tile([P, hi - lo], F32, "h_n4_%d_%d_%d" % (t, c, lo), "h_n4_%d_%d" % (t, lo))
+            window = h[t][:].indirect(n4_sb[:, (c * HALF + lo) // 16 : (c * HALF + hi) // 16])
+            if engine is None:
+                nc.vector.tensor_copy(h_n4[:], window)
+                nc.vector.scalar_tensor_tensor(res[c][:, t, lo:hi], h_n4[:], -0.5, big[t][:, lo:hi], ALU.mult, ALU.add)
+            else:
+                nc.scalar.activation(h_n4[:], window, ACT.Copy, scale=-0.5)
+                engine.tensor_tensor(res[c][:, t, lo:hi], h_n4[:], big[t][:, lo:hi], ALU.add)
+
+        def round_out(c, lo, hi, tag):
+            res_bf = tile([P, hi - lo, PACK], BF16, "res_bf%d_%d" % (c, lo), tag)
+            nc.vector.tensor_copy(res_bf[:].rearrange("p (g i) t -> p g t i", i=4),
+                                  res[c][:, :, lo:hi].rearrange("p t (g i) -> p g t i", i=4))
+            return res_bf
+
+        def quantise_out(c, lo, hi, res_bf):
+            cols = slice(c * HALF + lo, c * HALF + hi)
+            nc.vector.quantize_mx(out=ow[:, cols].bitcast(FP8X4), scales=osc[:, cols], in_=res_bf[:].rearrange("p j t -> p (j t)"))
+
         for c in range(2):
-            res = tile([P, PACK, HALF], F32, "res%d" % c)
+            big = []
             for t in range(PACK):
-                h_n4 = tile([P, HALF], F32, "h_n4_%d_%d" % (t, c))
-                ea = tile([P, HALF], F32, "ea_%d_%d" % (t, c))
-                big = tile([P, HALF], F32, "big_%d_%d" % (t, c))
-                nc.scalar.activation(h_n4[:], h[t][:].indirect(n4_sb[:, list_halves[c]]), ACT.Copy)
+                ea = tile([P, HALF], F32, "ea_%d_%d" % (t, c), "ea_%d" % t)
+                big.append(tile([P, HALF], F32, "big_%d_%d" % (t, c), "relay3" if (t, c) == (2, 1) else None))
+                early = tile([P, HALF], F32, "early", "h_n4_0_0") if (t, c) == (0, 0) else None
+                if early is not None:
+                    nc.scalar.activation(early[:], h[t][:].indirect(n4_sb[:, list_halves[c]]), ACT.Copy, scale=-0.5)
                 nc.scalar.activation(ea[:], h[t][:].indirect(n3_sb[:, list_halves[c]]), ACT.Exp,
                                      bias=shift[t][:], scale=tau_sb[:, t : t + 1])
-                nc.vector.scalar_tensor_tensor(big[:], ea[:], 2.0, h_ps[c][t][:, halves[0]], ALU.mult, ALU.max)
-                nc.vector.scalar_tensor_tensor(res[:, t, :], h_n4[:], -0.5, big[:], ALU.mult, ALU.add)
-            nc.sync.dma_start(out_rows[:, :, halves[c]], res[:])
-            res_bf = tile([P, HALF, PACK], BF16, "res_bf%d" % c)
-            nc.vector.tensor_copy(res_bf[:].rearrange("p (g i) t -> p g t i", i=4), res[:].rearrange("p t (g i) -> p g t i", i=4))
-            nc.vector.quantize_mx(out=ow[:, halves[c]].bitcast(FP8X4), scales=osc[:, halves[c]],
-                                  in_=res_bf[:].rearrange("p j t -> p (j t)"))
+                nc.vector.scalar_tensor_tensor(big[t][:], ea[:], 2.0, h_ps[t][:, halves[c]], ALU.mult, ALU.max)
+                if early is not None:
+                    nc.vector.tensor_tensor(res[c][:, t, :], early[:], big[t][:], ALU.add)
+                elif (t, c) == (3, 0):
+                    fetch_h(t, c, 0, HALF, None)
+                elif (t, c) == (3, 1):
+                    fetch_h(t, c, 0, P, nc.vector)
+                    fetch_h(t, c, P, HALF, nc.vector)
+                else:
+                    fetch_h(t, c, 0, HALF, nc.vector if (t, c) == (2, 1) else nc.vector)
+            nc.sync.dma_start(out_rows[:, :, halves[c]], res[c][:])
+            if c == 0:
+                quantise_out(c, 0, HALF, round_out(c, 0, HALF, "relay3"))
+            else:
+                pieces = [round_out(c, lo, lo + P, None) for lo in (0, P)]
+                for lo, piece in zip((0, P), pieces):
+                    quantise_out(c, lo, lo + P, piece)
             nc.sync.dma_start(out_words[:, halves[c]], ow[:, halves[c]].bitcast(I32))
         for q in range(4):
             queue = nc.scalar if q % 2 else nc.sync

@@ -14,11 +14,14 @@ ACT = mybir.ActivationFunctionType
 
 P = 128
 PACK = 4
+QUADS = 4
 S = 512
 T = 2048
 HALF = S // 2
-LIST_COLS = S // 16
-FLOPS = 3 * 2 * 512 * 512 * 512
+PER_COL = 16
+SPARE = 16
+LAST = PACK - 1
+FLOPS = 3 * 2 * S * S * S
 
 
 def tile_picked_twkeycrossbecl_none_po_kernel(
@@ -27,7 +30,11 @@ def tile_picked_twkeycrossbecl_none_po_kernel(
 ):
     nc = tc.nc
     halves = [slice(c * HALF, (c + 1) * HALF) for c in range(2)]
-    list_halves = [slice(c * LIST_COLS // 2, (c + 1) * LIST_COLS // 2) for c in range(2)]
+
+    def entries(lo, hi):
+        return slice(lo // PER_COL, hi // PER_COL)
+
+    half_entries = [entries(c * HALF, (c + 1) * HALF) for c in range(2)]
 
     with ExitStack() as ctx:
         keep = ctx.enter_context(tc.tile_pool(name="keep", bufs=1))
@@ -37,7 +44,7 @@ def tile_picked_twkeycrossbecl_none_po_kernel(
             return keep.tile(shape, dtype, name=name, tag=tag or name, align_bytes=64)
 
         def load_list(src, name):
-            dst = keep.tile([P, LIST_COLS], U16, name=name)
+            dst = keep.tile([P, S // PER_COL], U16, name=name)
             nc.sync.dma_start(dst[:], src)
             return dst
 
@@ -46,30 +53,37 @@ def tile_picked_twkeycrossbecl_none_po_kernel(
             nc.sync.dma_start(dst[:].bitcast(I32), src[0].rearrange("p n t -> p (n t)").bitcast(I32))
             return dst
 
-        def zeroed_plane(width, name, engine, tag=None):
+        def zeroed_bytes(width, name, tag=None):
             dst = tile([P, width], U8, name, tag)
-            engine.memset(dst[:].bitcast(I32), 0)
+            nc.vector.memset(dst[:].bitcast(I32), 0)
             return dst
 
-        def load_scale_rows(queue, dst, src):
-            for q in range(4):
-                queue.dma_start(dst[32 * q : 32 * q + 4, :].bitcast(I32), src[0, 4 * q : 4 * q + 4, :].bitcast(I32))
+        def load_scale_rows(dst, src):
+            for q in range(QUADS):
+                nc.sync.dma_start(dst[32 * q : 32 * q + 4, :].bitcast(I32), src[0, 4 * q : 4 * q + 4, :].bitcast(I32))
 
-        def dealt(ap):
-            return ap.rearrange("p (m t) -> p t m", t=PACK)
+        def deal_bytes(copy, dst, src):
+            copy(dst.rearrange("p (t m) -> p t m", t=PACK), src.rearrange("p (m t) -> p t m", t=PACK))
 
-        def as_dealt(ap):
-            return ap.rearrange("p (t m) -> p t m", t=PACK)
+        def deal_words(copy, dst, src):
+            copy(dst.rearrange("p (u v g i) -> p g u i v", u=2, v=2, i=4),
+                 src.rearrange("p (g i u v) -> p g u i v", u=2, v=2, i=4))
 
-        def mm(out, lw, ls, t, rw, rs):
+        def woven(ap):
+            return ap.rearrange("p (g i) t -> p g t i", i=2)
+
+        def apart(ap):
+            return ap.rearrange("p t (g i) -> p g t i", i=2)
+
+        def product(out, words, scales, t, moving_words, moving_scales):
             cols = slice(t * P, (t + 1) * P)
-            nc.tensor.matmul_mx(out=out, lhsT=lw[:, cols].bitcast(FP8X4), lhsT_scale=ls[:, cols],
-                                rhs=rw.bitcast(FP8X4), rhs_scale=rs, start=True, stop=True)
+            nc.tensor.matmul_mx(out=out, lhsT=words[:, cols].bitcast(FP8X4), lhsT_scale=scales[:, cols],
+                                rhs=moving_words.bitcast(FP8X4), rhs_scale=moving_scales, start=True, stop=True)
 
-        ds_table = zeroed_plane(T, "ds_table", nc.gpsimd)
-        w1s_raw = zeroed_plane(S, "w1s_raw", nc.vector, "relay")
-        ds_placed = zeroed_plane(S, "ds_placed", nc.vector)
-        w2s_raw = zeroed_plane(S, "w2s_raw", nc.vector)
+        ds_table = zeroed_bytes(T, "ds_table")
+        w1s_raw = zeroed_bytes(S, "w1s_raw", "w1s_then_ds")
+        ds_placed = zeroed_bytes(S, "ds_placed")
+        w2s_raw = zeroed_bytes(S, "w2s_raw")
 
         gn_sb = tile([P, PACK], F32, "gn_sb")
         nc.gpsimd.dma_start(gn_sb[:], gn.rearrange("(p t) o -> p (t o)", t=PACK))
@@ -78,48 +92,50 @@ def tile_picked_twkeycrossbecl_none_po_kernel(
 
         offs_sb = load_list(offs, "offs_sb")
         xs_table = tile([P, T], U8, "xs_table")
-        for q in range(4):
+        for q in range(QUADS):
             nc.sync.dma_start(xs_table[32 * q : 32 * q + 32, :].bitcast(I32),
                               x_scales[0, 4 * q : 4 * q + 4, :].bitcast(I32).partition_broadcast(8))
         k1_sb = load_list(k1, "k1_sb")
         nc.sync.dma_start(ds_table[0:P:8, :].bitcast(I32), d_scales[0].bitcast(I32))
         xw_table = load_words(x_words, T, "xw_table")
+        load_scale_rows(w1s_raw, w1_scales)
         w1w_raw = load_words(w1_words, S, "w1w_raw")
-        load_scale_rows(nc.sync, w1s_raw, w1_scales)
+        w2w_raw = load_words(w2_words, S, "w2w_raw")
         two_sb = load_list(two, "two_sb")
         dw_table = load_words(d_words, T, "dw_table")
         n1_sb = load_list(n1, "n1_sb")
         n2_sb = load_list(n2, "n2_sb")
-        w2w_raw = load_words(w2_words, S, "w2w_raw")
         n3_sb = load_list(n3, "n3_sb")
         n4_sb = load_list(n4, "n4_sb")
-        load_scale_rows(nc.sync, w2s_raw, w2_scales)
+        load_scale_rows(w2s_raw, w2_scales)
 
         gain = tile([P, PACK], F32, "gain")
         nc.scalar.activation(gain[:], gn_sb[:], ACT.Copy, scale=0.75 * 0.0625)
 
-        xs_idx = tile([P, S], U8, "xs_idx")
-        nc.vector.tensor_copy(xs_idx[:], xs_table[:].indirect(offs_sb[:]))
+        xs_offs = tile([P, S], U8, "xs_offs")
+        nc.vector.tensor_copy(xs_offs[:], xs_table[:].indirect(offs_sb[:]))
         ds_k1 = tile([P, S], U8, "ds_k1")
         nc.vector.tensor_copy(ds_k1[:], ds_table[:].indirect(k1_sb[:]))
         w1w = tile([P, S], U32, "w1w")
-        nc.scalar.copy(as_dealt(w1w[:]), dealt(w1w_raw[:]))
-        xw_idx = tile([P, S], U32, "xw_idx")
-        nc.vector.tensor_copy(xw_idx[:], xw_table[:].indirect(offs_sb[:]))
+        deal_words(nc.scalar.copy, w1w[:], w1w_raw[:])
+        w2w = tile([P, S], U32, "w2w")
+        deal_words(nc.scalar.copy, w2w[:], w2w_raw[:])
+        xw_offs = tile([P, S], U32, "xw_offs")
+        nc.vector.tensor_copy(xw_offs[:], xw_table[:].indirect(offs_sb[:]))
         w1s = tile([P, S], U8, "w1s")
-        nc.gpsimd.tensor_copy(as_dealt(w1s[:]), dealt(w1s_raw[:]))
+        deal_bytes(nc.gpsimd.tensor_copy, w1s[:], w1s_raw[:])
 
         y_ps = [psum.tile([P, S], F32, name="y_ps%d" % t, tag="bank%d" % t) for t in range(PACK)]
-        y = [tile([P, S + 16], F32, "y%d" % t) for t in range(PACK)]
+        y = [tile([P, S + SPARE], F32, "y%d" % t) for t in range(PACK)]
         for t in range(PACK):
             nc.vector.memset(y[t][:, S:], 0.0)
         for t in range(PACK):
-            mm(y_ps[t][:], w1w, w1s, t, xw_idx[:], xs_idx[:])
+            product(y_ps[t][:], w1w, w1s, t, xw_offs[:], xs_offs[:])
         for t in range(PACK):
             nc.scalar.copy(y[t][:, :S], y_ps[t][:])
 
-        ds_dealt = tile([P, S], U8, "ds_dealt", "relay")
-        nc.vector.tensor_copy(as_dealt(ds_dealt[:]), dealt(ds_k1[:]))
+        ds_dealt = tile([P, S], U8, "ds_dealt", "w1s_then_ds")
+        deal_bytes(nc.vector.tensor_copy, ds_dealt[:], ds_k1[:])
         for r in range(4):
             nc.sync.dma_start(ds_placed[r:P:32, :].bitcast(I32), ds_dealt[8 * r : P : 32, :].bitcast(I32))
         xs_two = tile([P, S], U8, "xs_two")
@@ -129,28 +145,23 @@ def tile_picked_twkeycrossbecl_none_po_kernel(
         dw_k1 = tile([P, S], U32, "dw_k1")
         nc.vector.tensor_copy(dw_k1[:], dw_table[:].indirect(k1_sb[:]))
         dw = tile([P, S], U32, "dw")
-        nc.vector.tensor_copy(as_dealt(dw[:]), dealt(dw_k1[:]))
-        w2w = tile([P, S], U32, "w2w")
-        nc.gpsimd.tensor_copy(as_dealt(w2w[:]), dealt(w2w_raw[:]))
-
+        deal_words(nc.vector.tensor_copy, dw[:], dw_k1[:])
         w2s = tile([P, S], U8, "w2s")
-        nc.gpsimd.tensor_copy(as_dealt(w2s[:]), dealt(w2s_raw[:]))
+        deal_bytes(nc.vector.tensor_copy, w2s[:], w2s_raw[:])
 
         d_ps = [psum.tile([P, S], F32, name="d_ps%d" % t, tag="bank%d" % (PACK + t)) for t in range(PACK)]
         for t in range(PACK):
-            mm(d_ps[t][:], dw, ds_placed, t, xw_two[:], xs_two[:])
+            product(d_ps[t][:], dw, ds_placed, t, xw_two[:], xs_two[:])
 
         y_n1 = [tile([P, S], F32, "y_n1_%d" % t) for t in range(PACK)]
         d = [tile([P, S], F32, "d%d" % t) for t in range(PACK)]
-        d_n2 = {(t, c): tile([P, HALF], F32, "d_n2_%d_%d" % (t, c), "d_n2_%d" % (t + c)) for c in range(2) for t in range(1 - c, PACK)}
+        d_n2 = {(t, c): tile([P, HALF], F32, "d_n2_%d_%d" % (t, c), "d_n2_%d" % (t + c))
+                for c in range(2) for t in range(1 - c, PACK)}
         left = [tile([P, PACK, HALF], F32, "left%d" % c, "left") for c in range(2)]
         right = [tile([P, PACK, HALF], F32, "right%d" % c) for c in range(2)]
 
-        def fetch_y(t):
-            nc.scalar.activation(y_n1[t][:], y[t][:].indirect(n1_sb[:]), ACT.Copy)
-
         for t in range(PACK):
-            fetch_y(t)
+            nc.scalar.activation(y_n1[t][:], y[t][:].indirect(n1_sb[:]), ACT.Copy)
         for t in range(PACK):
             nc.vector.tensor_scalar(d[t][:], d_ps[t][:], gain[:, t : t + 1], None, ALU.mult)
             nc.gpsimd.tensor_tensor(right[1][:, t, :], y_n1[t][:, halves[1]], d[t][:, halves[1]], ALU.mult)
@@ -164,21 +175,16 @@ def tile_picked_twkeycrossbecl_none_po_kernel(
         zs = [tile([P, HALF], U8, "zs%d" % c) for c in range(2)]
 
         def make_left(t, c):
-            nc.scalar.activation(d_n2[t, c][:], d[t][:].indirect(n2_sb[:, list_halves[c]]), ACT.Copy)
+            nc.scalar.activation(d_n2[t, c][:], d[t][:].indirect(n2_sb[:, half_entries[c]]), ACT.Copy)
             nc.vector.tensor_tensor(left[c][:, t, :], d_n2[t, c][:], y_ps[t][:, halves[c]], ALU.mult)
 
         def make_z(c):
-            nc.vector.tensor_tensor(
-                z[c][:].rearrange("p (g i) t -> p g t i", i=4),
-                left[c][:].rearrange("p t (g i) -> p g t i", i=4),
-                right[c][:].rearrange("p t (g i) -> p g t i", i=4),
-                ALU.subtract,
-            )
+            nc.vector.tensor_tensor(woven(z[c][:]), apart(left[c][:]), apart(right[c][:]), ALU.subtract)
 
         def second_product(c):
             nc.vector.quantize_mx(out=zw[c][:].bitcast(FP8X4), scales=zs[c][:], in_=z[c][:].rearrange("p j t -> p (j t)"))
             for t in range(PACK):
-                mm(h_ps[t][:, halves[c]], w2w, w2s, t, zw[c][:], zs[c][:])
+                product(h_ps[t][:, halves[c]], w2w, w2s, t, zw[c][:], zs[c][:])
 
         h = [tile([P, S], F32, "h%d" % t) for t in range(PACK)]
         top_half = [tile([P, 1], F32, "top_half_%d" % t) for t in range(2)]
@@ -191,7 +197,7 @@ def tile_picked_twkeycrossbecl_none_po_kernel(
         def make_shift(t):
             nc.vector.tensor_scalar(shift[t][:], top[t][:], tau_sb[:, t : t + 1], -1.0, ALU.mult, ALU.mult)
 
-        nc.vector.tensor_tensor(left[0][:, 0, :], d[0][:].indirect(n2_sb[:, list_halves[0]]), y[0][:, halves[0]], ALU.mult)
+        nc.vector.tensor_tensor(left[0][:, 0, :], d[0][:].indirect(n2_sb[:, half_entries[0]]), y[0][:, halves[0]], ALU.mult)
         for t in range(1, PACK):
             make_left(t, 0)
         make_z(0)
@@ -206,11 +212,10 @@ def tile_picked_twkeycrossbecl_none_po_kernel(
         take_h(0, halves[1], top_half[0][:], top[0][:])
         take_h(1, halves[1], top_half[1][:], top[1][:])
         make_shift(0)
-        take_h(2, slice(0, S), None, top[2][:])
-        make_shift(1)
-        take_h(3, slice(0, S), None, top[3][:])
-        make_shift(2)
-        make_shift(3)
+        for t in range(2, PACK):
+            take_h(t, slice(0, S), None, top[t][:])
+            make_shift(t - 1)
+        make_shift(LAST)
 
         out_rows = out_0.rearrange("(p t) j -> p t j", t=PACK)
         out_words = out_1[0].rearrange("p n t -> p (n t)").bitcast(I32)
@@ -218,54 +223,69 @@ def tile_picked_twkeycrossbecl_none_po_kernel(
         osc = tile([P, S], U8, "osc")
         res = [tile([P, PACK, HALF], F32, "res%d" % c) for c in range(2)]
 
-        def fetch_h(t, c, lo, hi, engine):
+        def fetch_n4(t, c, lo, hi, on_vector):
             h_n4 = tile([P, hi - lo], F32, "h_n4_%d_%d_%d" % (t, c, lo), "h_n4_%d_%d" % (t, lo))
-            window = h[t][:].indirect(n4_sb[:, (c * HALF + lo) // 16 : (c * HALF + hi) // 16])
-            if engine is None:
-                nc.vector.tensor_copy(h_n4[:], window)
-                nc.vector.scalar_tensor_tensor(res[c][:, t, lo:hi], h_n4[:], -0.5, big[t][:, lo:hi], ALU.mult, ALU.add)
+            looked_up = h[t][:].indirect(n4_sb[:, entries(c * HALF + lo, c * HALF + hi)])
+            if on_vector:
+                nc.vector.tensor_copy(h_n4[:], looked_up)
             else:
-                nc.scalar.activation(h_n4[:], window, ACT.Copy, scale=-0.5)
-                engine.tensor_tensor(res[c][:, t, lo:hi], h_n4[:], big[t][:, lo:hi], ALU.add)
+                nc.scalar.activation(h_n4[:], looked_up, ACT.Copy, scale=-0.5)
+            return h_n4
+
+        def larger(t, c):
+            ea = tile([P, HALF], F32, "ea_%d_%d" % (t, c), "ea_%d" % t)
+            big = tile([P, HALF], F32, "big_%d_%d" % (t, c), "planes0_then_big" if (t, c) == (2, 1) else None)
+            nc.scalar.activation(ea[:], h[t][:].indirect(n3_sb[:, half_entries[c]]), ACT.Exp,
+                                 bias=shift[t][:], scale=tau_sb[:, t : t + 1])
+            nc.vector.scalar_tensor_tensor(big[:], ea[:], 2.0, h_ps[t][:, halves[c]], ALU.mult, ALU.max)
+            return big
 
         def round_out(c, lo, hi, tag):
             res_bf = tile([P, hi - lo, PACK], BF16, "res_bf%d_%d" % (c, lo), tag)
-            nc.vector.tensor_copy(res_bf[:].rearrange("p (g i) t -> p g t i", i=4),
-                                  res[c][:, :, lo:hi].rearrange("p t (g i) -> p g t i", i=4))
+            nc.vector.tensor_copy(woven(res_bf[:]), apart(res[c][:, :, lo:hi]))
             return res_bf
 
         def quantise_out(c, lo, hi, res_bf):
             cols = slice(c * HALF + lo, c * HALF + hi)
             nc.vector.quantize_mx(out=ow[:, cols].bitcast(FP8X4), scales=osc[:, cols], in_=res_bf[:].rearrange("p j t -> p (j t)"))
 
-        for c in range(2):
-            big = []
-            for t in range(PACK):
-                ea = tile([P, HALF], F32, "ea_%d_%d" % (t, c), "ea_%d" % t)
-                big.append(tile([P, HALF], F32, "big_%d_%d" % (t, c), "relay3" if (t, c) == (2, 1) else None))
-                early = tile([P, HALF], F32, "early", "h_n4_0_0") if (t, c) == (0, 0) else None
-                if early is not None:
-                    nc.scalar.activation(early[:], h[t][:].indirect(n4_sb[:, list_halves[c]]), ACT.Copy, scale=-0.5)
-                nc.scalar.activation(ea[:], h[t][:].indirect(n3_sb[:, list_halves[c]]), ACT.Exp,
-                                     bias=shift[t][:], scale=tau_sb[:, t : t + 1])
-                nc.vector.scalar_tensor_tensor(big[t][:], ea[:], 2.0, h_ps[t][:, halves[c]], ALU.mult, ALU.max)
-                if early is not None:
-                    nc.vector.tensor_tensor(res[c][:, t, :], early[:], big[t][:], ALU.add)
-                elif (t, c) == (3, 0):
-                    fetch_h(t, c, 0, HALF, None)
-                elif (t, c) == (3, 1):
-                    fetch_h(t, c, 0, P, nc.vector)
-                    fetch_h(t, c, P, HALF, nc.vector)
-                else:
-                    fetch_h(t, c, 0, HALF, nc.vector if (t, c) == (2, 1) else nc.vector)
-            nc.sync.dma_start(out_rows[:, :, halves[c]], res[c][:])
-            if c == 0:
-                quantise_out(c, 0, HALF, round_out(c, 0, HALF, "relay3"))
-            else:
-                pieces = [round_out(c, lo, lo + P, None) for lo in (0, P)]
-                for lo, piece in zip((0, P), pieces):
-                    quantise_out(c, lo, lo + P, piece)
+        def store_rows(c, tiles):
+            nc.sync.dma_start(out_rows[:, tiles, halves[c]], res[c][:, tiles, :])
+
+        def store_words(c):
             nc.sync.dma_start(out_words[:, halves[c]], ow[:, halves[c]].bitcast(I32))
-        for q in range(4):
+
+        h_n4 = fetch_n4(0, 0, 0, HALF, False)
+        big = larger(0, 0)
+        nc.gpsimd.tensor_tensor(res[0][:, 0, :], h_n4[:], big[:], ALU.add)
+        for t in range(1, LAST):
+            big = larger(t, 0)
+            h_n4 = fetch_n4(t, 0, 0, HALF, False)
+            adder = nc.gpsimd if t == 1 else nc.vector
+            adder.tensor_tensor(res[0][:, t, :], h_n4[:], big[:], ALU.add)
+        big = larger(LAST, 0)
+        h_n4 = fetch_n4(LAST, 0, 0, HALF, True)
+        nc.vector.scalar_tensor_tensor(res[0][:, LAST, :], h_n4[:], -0.5, big[:], ALU.mult, ALU.add)
+        store_rows(0, slice(0, PACK))
+        quantise_out(0, 0, HALF, round_out(0, 0, HALF, "planes0_then_big"))
+        store_words(0)
+
+        quarters = [(0, HALF // 2), (HALF // 2, HALF)]
+        for t in range(LAST):
+            big = larger(t, 1)
+            h_n4 = fetch_n4(t, 1, 0, HALF, False)
+            nc.vector.tensor_tensor(res[1][:, t, :], h_n4[:], big[:], ALU.add)
+        store_rows(1, slice(0, LAST))
+        big = larger(LAST, 1)
+        for lo, hi in quarters:
+            h_n4 = fetch_n4(LAST, 1, lo, hi, False)
+            nc.vector.tensor_tensor(res[1][:, LAST, lo:hi], h_n4[:], big[:, lo:hi], ALU.add)
+        store_rows(1, slice(LAST, PACK))
+        rounded = [round_out(1, lo, hi, None) for lo, hi in quarters]
+        for (lo, hi), res_bf in zip(quarters, rounded):
+            quantise_out(1, lo, hi, res_bf)
+        store_words(1)
+
+        for q in range(QUADS):
             queue = nc.scalar if q % 2 else nc.sync
             queue.dma_start(out_2[0, 4 * q : 4 * q + 4, :].bitcast(I32), osc[32 * q : 32 * q + 4, :].bitcast(I32))

from contextlib import ExitStack

import concourse.mybir as mybir

F32 = mybir.dt.float32
BF16 = mybir.dt.bfloat16
I32 = mybir.dt.int32
U32 = mybir.dt.uint32
U16 = mybir.dt.uint16
U8 = mybir.dt.uint8
FP8X4 = mybir.dt.float8_e4m3fn_x4
ALU = mybir.AluOpType
ACT = mybir.ActivationFunctionType

P = 128
PACK = 4
QUADS = 4
S = 512
T = 2048
HALF = S // 2
PER_COL = 16
SPARE = 16
LAST = PACK - 1
FLOPS = 3 * 2 * S * S * S


def tile_picked_twkeycrossbecl_none_po_kernel(
    tc, x_words, x_scales, w1_words, w1_scales, d_words, d_scales, gn, w2_words, w2_scales, tau,
    offs, k1, two, n1, n2, n3, n4, out_0, out_1, out_2,
):
    nc = tc.nc
    halves = [slice(c * HALF, (c + 1) * HALF) for c in range(2)]

    def entries(lo, hi):
        return slice(lo // PER_COL, hi // PER_COL)

    half_entries = [entries(c * HALF, (c + 1) * HALF) for c in range(2)]

    with ExitStack() as ctx:
        keep = ctx.enter_context(tc.tile_pool(name="keep", bufs=1))
        psum = ctx.enter_context(tc.psum_pool(name="psum", bufs=1))

        def tile(shape, dtype, name, tag=None):
            return keep.tile(shape, dtype, name=name, tag=tag or name, align_bytes=64)

        def load_list(src, name):
            dst = keep.tile([P, S // PER_COL], U16, name=name)
            nc.sync.dma_start(dst[:], src)
            return dst

        def load_words(src, width, name):
            dst = tile([P, width], U32, name)
            nc.sync.dma_start(dst[:].bitcast(I32), src[0].rearrange("p n t -> p (n t)").bitcast(I32))
            return dst

        def zeroed_bytes(width, name, tag=None):
            dst = tile([P, width], U8, name, tag)
            nc.vector.memset(dst[:].bitcast(I32), 0)
            return dst

        def load_scale_rows(dst, src):
            for q in range(QUADS):
                nc.sync.dma_start(dst[32 * q : 32 * q + 4, :].bitcast(I32), src[0, 4 * q : 4 * q + 4, :].bitcast(I32))

        def deal_bytes(copy, dst, src):
            copy(dst.rearrange("p (t m) -> p t m", t=PACK), src.rearrange("p (m t) -> p t m", t=PACK))

        def deal_words(copy, dst, src):
            copy(dst.rearrange("p (u v g i) -> p g u i v", u=2, v=2, i=4),
                 src.rearrange("p (g i u v) -> p g u i v", u=2, v=2, i=4))

        def woven(ap):
            return ap.rearrange("p (g i) t -> p g t i", i=2)

        def apart(ap):
            return ap.rearrange("p t (g i) -> p g t i", i=2)

        def product(out, words, scales, t, moving_words, moving_scales):
            cols = slice(t * P, (t + 1) * P)
            nc.tensor.matmul_mx(out=out, lhsT=words[:, cols].bitcast(FP8X4), lhsT_scale=scales[:, cols],
                                rhs=moving_words.bitcast(FP8X4), rhs_scale=moving_scales, start=True, stop=True)

        ds_table = zeroed_bytes(T, "ds_table")
        w1s_raw = zeroed_bytes(S, "w1s_raw", "w1s_then_ds")
        ds_placed = zeroed_bytes(S, "ds_placed")
        w2s_raw = zeroed_bytes(S, "w2s_raw")

        gn_sb = tile([P, PACK], F32, "gn_sb")
        nc.gpsimd.dma_start(gn_sb[:], gn.rearrange("(p t) o -> p (t o)", t=PACK))
        tau_sb = tile([P, PACK], F32, "tau_sb")
        nc.gpsimd.dma_start(tau_sb[:], tau.rearrange("(p t) o -> p (t o)", t=PACK))

        offs_sb = load_list(offs, "offs_sb")
        xs_table = tile([P, T], U8, "xs_table")
        for q in range(QUADS):
            nc.sync.dma_start(xs_table[32 * q : 32 * q + 32, :].bitcast(I32),
                              x_scales[0, 4 * q : 4 * q + 4, :].bitcast(I32).partition_broadcast(8))
        k1_sb = load_list(k1, "k1_sb")
        nc.sync.dma_start(ds_table[0:P:8, :].bitcast(I32), d_scales[0].bitcast(I32))
        xw_table = load_words(x_words, T, "xw_table")
        load_scale_rows(w1s_raw, w1_scales)
        w1w_raw = load_words(w1_words, S, "w1w_raw")
        w2w_raw = load_words(w2_words, S, "w2w_raw")
        two_sb = load_list(two, "two_sb")
        dw_table = load_words(d_words, T, "dw_table")
        n1_sb = load_list(n1, "n1_sb")
        n2_sb = load_list(n2, "n2_sb")
        n3_sb = load_list(n3, "n3_sb")
        n4_sb = load_list(n4, "n4_sb")
        load_scale_rows(w2s_raw, w2_scales)

        gain = tile([P, PACK], F32, "gain")
        nc.scalar.activation(gain[:], gn_sb[:], ACT.Copy, scale=0.75 * 0.0625)

        xs_offs = tile([P, S], U8, "xs_offs")
        nc.vector.tensor_copy(xs_offs[:], xs_table[:].indirect(offs_sb[:]))
        ds_k1 = tile([P, S], U8, "ds_k1")
        nc.vector.tensor_copy(ds_k1[:], ds_table[:].indirect(k1_sb[:]))
        w1w = tile([P, S], U32, "w1w")
        deal_words(nc.scalar.copy, w1w[:], w1w_raw[:])
        w2w = tile([P, S], U32, "w2w")
        deal_words(nc.scalar.copy, w2w[:], w2w_raw[:])
        xw_offs = tile([P, S], U32, "xw_offs")
        nc.vector.tensor_copy(xw_offs[:], xw_table[:].indirect(offs_sb[:]))
        w1s = tile([P, S], U8, "w1s")
        deal_bytes(nc.gpsimd.tensor_copy, w1s[:], w1s_raw[:])

        y_ps = [psum.tile([P, S], F32, name="y_ps%d" % t, tag="bank%d" % t) for t in range(PACK)]
        y = [tile([P, S + SPARE], F32, "y%d" % t) for t in range(PACK)]
        for t in range(PACK):
            nc.vector.memset(y[t][:, S:], 0.0)
        for t in range(PACK):
            product(y_ps[t][:], w1w, w1s, t, xw_offs[:], xs_offs[:])
        for t in range(PACK):
            nc.scalar.copy(y[t][:, :S], y_ps[t][:])

        ds_dealt = tile([P, S], U8, "ds_dealt", "w1s_then_ds")
        deal_bytes(nc.vector.tensor_copy, ds_dealt[:], ds_k1[:])
        for r in range(4):
            nc.sync.dma_start(ds_placed[r:P:32, :].bitcast(I32), ds_dealt[8 * r : P : 32, :].bitcast(I32))
        xs_two = tile([P, S], U8, "xs_two")
        nc.vector.tensor_copy(xs_two[:], xs_table[:].indirect(two_sb[:]))
        xw_two = tile([P, S], U32, "xw_two")
        nc.vector.tensor_copy(xw_two[:], xw_table[:].indirect(two_sb[:]))
        dw_k1 = tile([P, S], U32, "dw_k1")
        nc.vector.tensor_copy(dw_k1[:], dw_table[:].indirect(k1_sb[:]))
        dw = tile([P, S], U32, "dw")
        deal_words(nc.vector.tensor_copy, dw[:], dw_k1[:])
        w2s = tile([P, S], U8, "w2s")
        deal_bytes(nc.vector.tensor_copy, w2s[:], w2s_raw[:])

        d_ps = [psum.tile([P, S], F32, name="d_ps%d" % t, tag="bank%d" % (PACK + t)) for t in range(PACK)]
        for t in range(PACK):
            product(d_ps[t][:], dw, ds_placed, t, xw_two[:], xs_two[:])

        y_n1 = [tile([P, S], F32, "y_n1_%d" % t) for t in range(PACK)]
        d = [tile([P, S], F32, "d%d" % t) for t in range(PACK)]
        d_n2 = {(t, c): tile([P, HALF], F32, "d_n2_%d_%d" % (t, c), "d_n2_%d" % (t + c))
                for c in range(2) for t in range(1 - c, PACK)}
        left = [tile([P, PACK, HALF], F32, "left%d" % c, "left") for c in range(2)]
        right = [tile([P, PACK, HALF], F32, "right%d" % c) for c in range(2)]

        for t in range(PACK):
            nc.scalar.activation(y_n1[t][:], y[t][:].indirect(n1_sb[:]), ACT.Copy)
        for t in range(PACK):
            nc.vector.tensor_scalar(d[t][:], d_ps[t][:], gain[:, t : t + 1], None, ALU.mult)
            nc.gpsimd.tensor_tensor(right[1][:, t, :], y_n1[t][:, halves[1]], d[t][:, halves[1]], ALU.mult)
        for t in range(PACK):
            nc.vector.scalar_tensor_tensor(right[0][:, t, :], d_ps[t][:, halves[0]], gain[:, t : t + 1],
                                           y_n1[t][:, halves[0]], ALU.mult, ALU.mult)

        h_ps = [psum.tile([P, S], F32, name="h_ps%d" % t, tag="bank%d" % (PACK + t)) for t in range(PACK)]
        z = [tile([P, HALF, PACK], BF16, "z%d" % c) for c in range(2)]
        zw = [tile([P, HALF], U32, "zw%d" % c) for c in range(2)]
        zs = [tile([P, HALF], U8, "zs%d" % c) for c in range(2)]

        def make_left(t, c):
            nc.scalar.activation(d_n2[t, c][:], d[t][:].indirect(n2_sb[:, half_entries[c]]), ACT.Copy)
            nc.vector.tensor_tensor(left[c][:, t, :], d_n2[t, c][:], y_ps[t][:, halves[c]], ALU.mult)

        def make_z(c):
            nc.vector.tensor_tensor(woven(z[c][:]), apart(left[c][:]), apart(right[c][:]), ALU.subtract)

        def second_product(c):
            nc.vector.quantize_mx(out=zw[c][:].bitcast(FP8X4), scales=zs[c][:], in_=z[c][:].rearrange("p j t -> p (j t)"))
            for t in range(PACK):
                product(h_ps[t][:, halves[c]], w2w, w2s, t, zw[c][:], zs[c][:])

        h = [tile([P, S], F32, "h%d" % t) for t in range(PACK)]
        top_half = [tile([P, 1], F32, "top_half_%d" % t) for t in range(2)]
        top = [tile([P, 1], F32, "top_%d" % t) for t in range(PACK)]
        shift = [tile([P, 1], F32, "shift_%d" % t) for t in range(PACK)]

        def take_h(t, cols, so_far, largest):
            nc.vector.tensor_scalar(h[t][:, cols], h_ps[t][:, cols], 1.0, so_far, ALU.mult, ALU.max, accum_out=largest)

        def make_shift(t):
            nc.vector.tensor_scalar(shift[t][:], top[t][:], tau_sb[:, t : t + 1], -1.0, ALU.mult, ALU.mult)

        nc.vector.tensor_tensor(left[0][:, 0, :], d[0][:].indirect(n2_sb[:, half_entries[0]]), y[0][:, halves[0]], ALU.mult)
        for t in range(1, PACK):
            make_left(t, 0)
        make_z(0)
        make_left(0, 1)
        second_product(0)
        for t in range(1, PACK):
            make_left(t, 1)
        take_h(0, halves[0], None, top_half[0][:])
        make_z(1)
        take_h(1, halves[0], None, top_half[1][:])
        second_product(1)
        take_h(0, halves[1], top_half[0][:], top[0][:])
        take_h(1, halves[1], top_half[1][:], top[1][:])
        make_shift(0)
        for t in range(2, PACK):
            take_h(t, slice(0, S), None, top[t][:])
            make_shift(t - 1)
        make_shift(LAST)

        out_rows = out_0.rearrange("(p t) j -> p t j", t=PACK)
        out_words = out_1[0].rearrange("p n t -> p (n t)").bitcast(I32)
        ow = tile([P, S], U32, "ow")
        osc = tile([P, S], U8, "osc")
        res = [tile([P, PACK, HALF], F32, "res%d" % c) for c in range(2)]

        def fetch_n4(t, c, lo, hi, on_vector):
            h_n4 = tile([P, hi - lo], F32, "h_n4_%d_%d_%d" % (t, c, lo), "h_n4_%d_%d" % (t, lo))
            looked_up = h[t][:].indirect(n4_sb[:, entries(c * HALF + lo, c * HALF + hi)])
            if on_vector:
                nc.vector.tensor_copy(h_n4[:], looked_up)
            else:
                nc.scalar.activation(h_n4[:], looked_up, ACT.Copy, scale=-0.5)
            return h_n4

        def larger(t, c):
            ea = tile([P, HALF], F32, "ea_%d_%d" % (t, c), "ea_%d" % t)
            big = tile([P, HALF], F32, "big_%d_%d" % (t, c), "planes0_then_big" if (t, c) == (2, 1) else None)
            nc.scalar.activation(ea[:], h[t][:].indirect(n3_sb[:, half_entries[c]]), ACT.Exp,
                                 bias=shift[t][:], scale=tau_sb[:, t : t + 1])
            nc.vector.scalar_tensor_tensor(big[:], ea[:], 2.0, h_ps[t][:, halves[c]], ALU.mult, ALU.max)
            return big

        def round_out(c, lo, hi, tag):
            res_bf = tile([P, hi - lo, PACK], BF16, "res_bf%d_%d" % (c, lo), tag)
            nc.vector.tensor_copy(woven(res_bf[:]), apart(res[c][:, :, lo:hi]))
            return res_bf

        def quantise_out(c, lo, hi, res_bf):
            cols = slice(c * HALF + lo, c * HALF + hi)
            nc.vector.quantize_mx(out=ow[:, cols].bitcast(FP8X4), scales=osc[:, cols], in_=res_bf[:].rearrange("p j t -> p (j t)"))

        def store_rows(c, tiles):
            nc.sync.dma_start(out_rows[:, tiles, halves[c]], res[c][:, tiles, :])

        def store_words(c):
            nc.sync.dma_start(out_words[:, halves[c]], ow[:, halves[c]].bitcast(I32))

        h_n4 = fetch_n4(0, 0, 0, HALF, False)
        big = larger(0, 0)
        nc.gpsimd.tensor_tensor(res[0][:, 0, :], h_n4[:], big[:], ALU.add)
        for t in range(1, LAST):
            big = larger(t, 0)
            h_n4 = fetch_n4(t, 0, 0, HALF, False)
            adder = nc.gpsimd if t == 1 else nc.vector
            adder.tensor_tensor(res[0][:, t, :], h_n4[:], big[:], ALU.add)
        big = larger(LAST, 0)
        h_n4 = fetch_n4(LAST, 0, 0, HALF, True)
        nc.vector.scalar_tensor_tensor(res[0][:, LAST, :], h_n4[:], -0.5, big[:], ALU.mult, ALU.add)
        store_rows(0, slice(0, PACK))
        quantise_out(0, 0, HALF, round_out(0, 0, HALF, "planes0_then_big"))
        store_words(0)

        quarters = [(0, HALF // 2), (HALF // 2, HALF)]
        for t in range(LAST):
            big = larger(t, 1)
            h_n4 = fetch_n4(t, 1, 0, HALF, False)
            nc.vector.tensor_tensor(res[1][:, t, :], h_n4[:], big[:], ALU.add)
        store_rows(1, slice(0, LAST))
        big = larger(LAST, 1)
        for lo, hi in quarters:
            h_n4 = fetch_n4(LAST, 1, lo, hi, False)
            nc.vector.tensor_tensor(res[1][:, LAST, lo:hi], h_n4[:], big[:, lo:hi], ALU.add)
        store_rows(1, slice(LAST, PACK))
        rounded = [round_out(1, lo, hi, None) for lo, hi in quarters]
        for (lo, hi), res_bf in zip(quarters, rounded):
            quantise_out(1, lo, hi, res_bf)
        store_words(1)

        for q in range(QUADS):
            queue = nc.scalar if q % 2 else nc.sync
            queue.dma_start(out_2[0, 4 * q : 4 * q + 4, :].bitcast(I32), osc[32 * q : 32 * q + 4, :].bitcast(I32))
